import numpy as np
import ml_dtypes


def mxq(x, axis, fmt="e4m3"):
    dtype, down = {"e4m3": (ml_dtypes.float8_e4m3fn, 7), "e5m2": (ml_dtypes.float8_e5m2, 14)}[fmt]
    v = np.moveaxis(np.asarray(x, np.float32).astype(ml_dtypes.bfloat16).astype(np.float64), axis, -1)
    blocks = v.reshape(v.shape[:-1] + (-1, 32))
    amax = np.abs(blocks).max(-1, keepdims=True)
    byte = np.maximum(np.where(amax > 0, np.frexp(amax)[1] - 1 + 127, 0) - down, 1)
    scale = np.exp2(byte - 127.0)
    codes = (blocks / scale).astype(np.float32).astype(dtype).astype(np.float64)
    return np.moveaxis((codes * scale).reshape(v.shape), -1, axis)


WIDE = False


def mx_kscale(k):
    if not WIDE:
        return np.ones(k)
    levels = np.array([10, -10, 5, -5, 0])
    if k % 512:
        return np.exp2(np.random.permutation(np.resize(levels, k // 32))).repeat(32)
    a = np.empty((k // 512, 16))
    for p in range(k // 512):
        a[p, :8] = np.random.permutation(np.resize(levels, 8))
        for g in range(8):
            far = levels[np.abs(levels - a[p, g]) >= 10]
            a[p, g + 8] = far[np.random.randint(len(far))]
    return np.exp2(a.ravel()).repeat(32)


def f64(x):
    return np.asarray(x).astype(np.float64)


def striped(idx):
    return np.tile(idx.reshape(-1, 16).T, (8, 1)).astype(np.uint16)


def unstriped(offs):
    return offs[:16].T.reshape(-1).astype(np.int64)


def pack_weight(w):
    k, n = w.shape
    w = f64(np.asarray(w, np.float32).astype(ml_dtypes.bfloat16)).reshape(k // 32, 32, n)
    amax = np.abs(w).max(1)
    byte = np.clip(np.where(amax > 0, np.frexp(amax)[1] - 1 + 127 - 7, 1), 1, 254)
    scaled = (w * np.exp2(127.0 - byte)[:, None, :]).reshape(k, n).astype(np.float32)
    words = np.ascontiguousarray(scaled.reshape(k // 512, 128, 4, n).transpose(0, 1, 3, 2)).astype(ml_dtypes.float8_e4m3fn).view(np.uint8)
    return words, np.ascontiguousarray(byte.astype(np.uint8).reshape(k // 512, 16, n))


def unpack_weight(words, scales):
    g, p, n, _ = words.shape
    vals = np.ascontiguousarray(words).view(ml_dtypes.float8_e4m3fn).astype(np.float64) * np.repeat(np.exp2(scales.astype(np.float64) - 127.0), 8, axis=1)[..., None]
    return vals.transpose(0, 1, 3, 2).reshape(g * 512, n)


E2M1 = np.array([0.0, 0.5, 1.0, 1.5, 2.0, 3.0, 4.0, 6.0, -0.0, -0.5, -1.0, -1.5, -2.0, -3.0, -4.0, -6.0])


def pack_fp4(w):
    k, n = w.shape
    w = f64(np.asarray(w, np.float32).astype(ml_dtypes.bfloat16)).reshape(k // 32, 32, n)
    amax = np.abs(w).max(1)
    mant, ex = np.frexp(amax / 6.0)
    byte = np.clip(np.where(amax > 0, np.where(mant > 0.5, ex, ex - 1) + 127, 1), 1, 254)
    scaled = (w * np.exp2(127.0 - byte)[:, None, :]).reshape(k, n).astype(np.float32)
    c = np.ascontiguousarray(scaled.reshape(k // 512, 128, 4, n).transpose(0, 1, 3, 2)).astype(ml_dtypes.float4_e2m1fn).view(np.uint8) & 0xF
    words = (c[..., 0::2] | (c[..., 1::2] << 4)).reshape(k // 512, 128, 2 * n)
    return np.ascontiguousarray(words), np.ascontiguousarray(byte.astype(np.uint8).reshape(k // 512, 16, n))


def unpack_fp4(words, scales):
    g, _, n = scales.shape
    words = np.ascontiguousarray(words).reshape(g, 128, n, 2)
    nib = np.empty((g, 128, n, 4), np.uint8)
    nib[..., 0::2] = words & 0xF
    nib[..., 1::2] = words >> 4
    vals = E2M1[nib] * np.repeat(np.exp2(scales.astype(np.float64) - 127.0), 8, axis=1)[..., None]
    return vals.transpose(0, 1, 3, 2).reshape(g * 512, n)


def planes(y):
    n, m = y.shape
    v = y.astype(np.float32).astype(ml_dtypes.bfloat16).astype(np.float64).reshape(n // 32, 32, m)
    top = np.abs(v).max(1)
    byte = np.clip(np.where(top > 0, np.frexp(top)[1] - 1 + 127 - 7, 1), 1, 254)
    codes = (v * np.exp2(127.0 - byte)[:, None, :]).reshape(n, m).astype(np.float32).astype(ml_dtypes.float8_e4m3fn).view(np.uint8)
    words = codes.reshape(n // 512, 128, 4, m).transpose(0, 1, 3, 2)
    return np.ascontiguousarray(words), np.ascontiguousarray(byte.astype(np.uint8).reshape(n // 512, 16, m))


K, T, S, N, H, U = 1024, 1024, 512, 512, 512, 1024


def setup_inputs():
    n = np.random.standard_normal
    s = mx_kscale(K)[:, None]
    u = mx_kscale(H)
    packed_xT = pack_weight(n((K, T)) * s)
    packed_w1 = pack_fp4(n((K, N)) / np.sqrt(K) / s)
    packed_w2 = pack_fp4(n((K, N)) / np.sqrt(K) / s)
    packed_w3 = pack_fp4(n((H, N)) / np.sqrt(H) / u[:, None])
    return {
        "x_words": packed_xT[0],
        "x_scales": packed_xT[1],
        "w1_words": packed_w1[0],
        "w1_scales": packed_w1[1],
        "w2_words": packed_w2[0],
        "w2_scales": packed_w2[1],
        "unit": (np.random.uniform(0.6, 1.4, (H, 1)) * u[:, None]).astype(np.float32),
        "w3_words": packed_w3[0],
        "w3_scales": packed_w3[1],
        "offs": striped(np.random.permutation(T)[:S]),
        "hl": striped(np.random.permutation(np.concatenate([np.arange(S), np.random.randint(0, S, U - S)]))),
        "wt": striped(np.random.permutation(np.concatenate([np.arange(S), np.random.randint(0, S, U - S)]))),
    }


def reference(x_words, x_scales, w1_words, w1_scales, w2_words, w2_scales, unit, w3_words, w3_scales, offs, hl, wt):
    xq = unpack_weight(x_words, x_scales)[:, unstriped(offs)]
    y = unpack_fp4(w1_words, w1_scales).T @ xq
    yh = y[:, unstriped(hl)]
    yw = y[:, unstriped(wt)]
    till = yh * yw
    z1 = unpack_fp4(w2_words, w2_scales).T @ xq
    zh = z1[:, unstriped(hl)]
    zw = z1[:, unstriped(wt)]
    hid = f64(unit) * (till - np.maximum(zh, zw))
    out_0 = unpack_fp4(w3_words, w3_scales).T @ mxq(hid, 0, "e4m3")
    return (out_0,) + planes(out_0)

@@ -1,0 +1,252 @@
+from contextlib import ExitStack
+
+import concourse.mybir as mybir
+
+F32 = mybir.dt.float32
+BF16 = mybir.dt.bfloat16
+I32 = mybir.dt.int32
+U32 = mybir.dt.uint32
+U16 = mybir.dt.uint16
+U8 = mybir.dt.uint8
+FP8X4 = mybir.dt.float8_e4m3fn_x4
+FP4X4 = mybir.dt.float4_e2m1fn_x4
+ACT = mybir.ActivationFunctionType
+ALU = mybir.AluOpType
+
+K, T, S, N, H, U = 1024, 1024, 512, 512, 512, 1024
+FLOPS = 2 * (2 * K * N * S + H * N * U)
+
+P = 128
+PACK = 4
+QUADS = 4
+PASSES = K // 512
+CHUNKS = [(0, 384, True), (384, 256, False), (640, 256, False), (896, 128, False)]
+PIECES = [(0, 0, 128), (0, 128, 256), (1, 0, 256), (2, 0, 256), (3, 0, 128)]
+TINY = 2.0 ** -100
+
+
+def load_scales(queue, plane, scales):
+    for q in range(QUADS):
+        queue.dma_start(
+            out=plane[32 * q : 32 * q + 4].bitcast(I32),
+            in_=scales[:, 4 * q : 4 * q + 4, :].rearrange("g r n -> r g n").bitcast(I32),
+        )
+
+
+def tile_picked_yleaseq_max_po_kernel(
+    tc, x_words, x_scales, w1_words, w1_scales, w2_words, w2_scales, unit, w3_words, w3_scales, offs, hl, wt,
+    out_0, out_1, out_2,
+):
+    nc = tc.nc
+    with ExitStack() as ctx:
+        lists = ctx.enter_context(tc.tile_pool(name="lists", bufs=1))
+        keep = ctx.enter_context(tc.tile_pool(name="keep", bufs=1))
+        heads = ctx.enter_context(tc.tile_pool(name="heads", bufs=4))
+        pairs = ctx.enter_context(tc.tile_pool(name="pairs", bufs=2))
+        psum = ctx.enter_context(tc.psum_pool(name="psum", bufs=8))
+
+        offs_sb = lists.tile([P, S // 16], U16, name="offs_sb")
+        hl_sb = lists.tile([P, U // 16], U16, name="hl_sb")
+        wt_sb = lists.tile([P, U // 16], U16, name="wt_sb")
+
+        xs_raw = keep.tile([P, PASSES, T], U8, name="xs_raw", align_bytes=64)
+        nc.vector.memset(xs_raw[:].bitcast(I32), 0)
+        ws_raw = []
+        for name, passes in (("w1", PASSES), ("w2", PASSES), ("w3", 1)):
+            plane = keep.tile([P, passes, N], U8, name=name + "s_raw", align_bytes=64)
+            nc.gpsimd.memset(plane[:].bitcast(I32), 0)
+            ws_raw.append(plane)
+
+        x_raw = [keep.tile([P, T], I32, name="x_raw%d" % g, align_bytes=64) for g in range(PASSES)]
+        w_raw = [
+            keep.tile([P, passes, 2 * N], U8, name=name + "_raw", align_bytes=64)
+            for name, passes in (("w1", PASSES), ("w2", PASSES), ("w3", 1))
+        ]
+        unit_sb = keep.tile([P, PACK], F32, name="unit_sb")
+
+        def load_words(i, words):
+            nc.sync.dma_start(out=w_raw[i][:].bitcast(I32), in_=words.rearrange("g p n -> p g n").bitcast(I32))
+
+        def load_x(g):
+            nc.sync.dma_start(out=x_raw[g][:], in_=x_words[g].rearrange("p n t -> p (n t)").bitcast(I32))
+
+        nc.sync.dma_start(offs_sb[:], offs)
+        load_x(0)
+        load_scales(nc.sync, xs_raw, x_scales)
+        load_x(1)
+        load_words(0, w1_words)
+        load_scales(nc.sync, ws_raw[0], w1_scales)
+        nc.sync.dma_start(out=unit_sb[:], in_=unit.rearrange("(p t) o -> p (t o)", t=PACK))
+        nc.sync.dma_start(hl_sb[:], hl)
+        load_words(1, w2_words)
+        nc.sync.dma_start(wt_sb[:], wt)
+        load_scales(nc.sync, ws_raw[1], w2_scales)
+        load_words(2, w3_words)
+        load_scales(nc.sync, ws_raw[2], w3_scales)
+
+        mag = keep.tile([P, PACK], F32, name="mag")
+        neg_mag = keep.tile([P, PACK], F32, name="neg_mag")
+        sign = keep.tile([P, PACK], BF16, name="sign")
+        nc.scalar.activation(mag[:], unit_sb[:], ACT.Abs)
+        nc.scalar.activation(neg_mag[:], mag[:], ACT.Copy, scale=-1.0)
+        nc.scalar.activation(sign[:], unit_sb[:], ACT.Sign)
+        guess = keep.tile([P, PACK], F32, name="guess")
+        twice = keep.tile([P, PACK], F32, name="twice")
+        inverse = keep.tile([P, PACK], F32, name="inverse")
+        half_quotient = keep.tile([P, PACK], F32, name="half_quotient")
+        root = keep.tile([P, PACK], F32, name="root")
+        nc.scalar.activation(guess[:], mag[:], ACT.Sqrt)
+        nc.vector.tensor_scalar(twice[:], guess[:], 2.0, TINY, ALU.mult, ALU.max)
+        nc.vector.reciprocal(inverse[:], twice[:])
+        nc.vector.tensor_tensor(half_quotient[:], mag[:], inverse[:], ALU.mult)
+        nc.vector.scalar_tensor_tensor(root[:], guess[:], 0.5, half_quotient[:], ALU.mult, ALU.add)
+
+        dealt = {}
+
+        def deal(i, t0, t1):
+            passes = w_raw[i].shape[1]
+            words = keep.tile([P, passes, t1 - t0, 2 * P], U8, name="wd%d_%d" % (i, t0), align_bytes=64)
+            scales = keep.tile([P, passes, t1 - t0, P], U8, name="sd%d_%d" % (i, t0), align_bytes=64)
+            nc.vector.tensor_copy(
+                out=words[:].bitcast(U16),
+                in_=w_raw[i][:].bitcast(U16).rearrange("p g (m t) -> p g t m", t=PACK)[:, :, t0:t1, :],
+            )
+            nc.vector.tensor_copy(
+                out=scales[:],
+                in_=ws_raw[i][:].rearrange("p g (m t) -> p g t m", t=PACK)[:, :, t0:t1, :],
+            )
+            for t in range(t0, t1):
+                dealt[(i, t)] = (words, scales, t - t0)
+
+        xs = [keep.tile([P, S], U8, name="xs%d" % g, align_bytes=64) for g in range(PASSES)]
+        xq = [keep.tile([P, S], U32, name="xq%d" % g, align_bytes=64) for g in range(PASSES)]
+        for g in range(PASSES):
+            nc.vector.tensor_copy(xs[g][:], xs_raw[:, g, :].indirect(offs_sb[:]))
+        deal(0, 0, 1)
+        for g in range(PASSES):
+            nc.vector.tensor_copy(xq[g][:], x_raw[g][:].bitcast(U32).indirect(offs_sb[:]))
+        deal(0, 1, PACK)
+        deal(1, 0, 1)
+        deal(1, 1, PACK)
+
+        def product(acc, i, t, g, codes, scale_plane, start, stop):
+            words, scales, j = dealt[(i, t)]
+            nc.tensor.matmul_mx(
+                out=acc,
+                lhsT=words[:, g, j, :].bitcast(FP4X4),
+                lhsT_scale=scales[:, g, j, :],
+                rhs=codes.bitcast(FP8X4),
+                rhs_scale=scale_plane,
+                start=start,
+                stop=stop,
+            )
+
+        y = [keep.tile([P, S], F32, name="y%d" % t) for t in range(PACK)]
+        z = [keep.tile([P, S], F32, name="z%d" % t) for t in range(PACK)]
+
+        def project(i, t):
+            acc = psum.tile([P, S], F32, name="acc")
+            for g in range(PASSES):
+                product(acc[:], i, t, g, xq[g][:], xs[g][:], g == 0, g == PASSES - 1)
+            if i == 0:
+                nc.scalar.activation(y[t][:], acc[:], ACT.Copy, scale=root[:, t : t + 1])
+            else:
+                nc.scalar.activation(z[t][:], acc[:], ACT.Copy, scale=neg_mag[:, t : t + 1])
+
+        out_scales = keep.tile([P, U], U8, name="out_scales", align_bytes=64)
+        out_rows = out_0.rearrange("(p t) r -> p t r", t=PACK)
+        out_words = out_1[0].rearrange("p r t -> p (r t)").bitcast(I32)
+
+        def side_by_side(tile):
+            return tile[:].rearrange("p (c i) t -> p c t i", i=4)
+
+        def by_slot(ap):
+            return ap.rearrange("p t (c i) -> p c t i", i=4)
+
+        stage = {}
+        held = {}
+
+        def fetch(c, t):
+            r0, n, fused = CHUNKS[c]
+            if t == 0:
+                names = ("till", "a", "b") if fused else ("till", "m")
+                stage[c] = [keep.tile([P, PACK, n], F32, name="%s%d" % (name, c)) for name in names]
+            till = stage[c][0]
+            h_list = hl_sb[:, r0 // 16 : (r0 + n) // 16]
+            w_list = wt_sb[:, r0 // 16 : (r0 + n) // 16]
+            yh = heads.tile([P, n], F32, name="yh")
+            nc.scalar.activation(yh[:], y[t][:].indirect(h_list), ACT.Copy)
+            nc.vector.tensor_tensor(till[:, t, :], y[t][:].indirect(w_list), yh[:], ALU.mult)
+            if fused:
+                nc.vector.tensor_tensor(stage[c][1][:, t, :], z[t][:].indirect(h_list), till[:, t, :], ALU.add)
+                nc.vector.tensor_tensor(stage[c][2][:, t, :], z[t][:].indirect(w_list), till[:, t, :], ALU.add)
+            else:
+                if t % 2 == 0:
+                    held[c] = [pairs.tile([P, 2, n], F32, name=name) for name in ("zh", "zw")]
+                zh, zw = held[c]
+                nc.scalar.activation(zh[:, t % 2, :], z[t][:].indirect(h_list), ACT.Copy)
+                nc.scalar.activation(zw[:, t % 2, :], z[t][:].indirect(w_list), ACT.Copy)
+                if t % 2 == 1:
+                    nc.vector.tensor_tensor(stage[c][1][:, t - 1 : t + 1, :], zh[:], zw[:], ALU.min)
+
+        results = {}
+
+        def finish(k):
+            c, a0, n = PIECES[k]
+            cols = slice(a0, a0 + n)
+            unsigned = keep.tile([P, n, PACK], BF16, name="unsigned%d" % k, align_bytes=64)
+            if CHUNKS[c][2]:
+                till, a, b = stage[c]
+                nc.vector.tensor_tensor(side_by_side(unsigned), by_slot(a[:, :, cols]), by_slot(b[:, :, cols]), ALU.min)
+            else:
+                till, m = stage[c]
+                nc.vector.tensor_tensor(side_by_side(unsigned), by_slot(till[:, :, cols]), by_slot(m[:, :, cols]), ALU.add)
+            hid = keep.tile([P, n, PACK], BF16, name="hid%d" % k, align_bytes=64)
+            nc.vector.tensor_tensor(hid[:], unsigned[:], sign[:].unsqueeze(1).to_broadcast([P, n, PACK]), ALU.mult)
+            hq = keep.tile([P, n], U32, name="hq%d" % k, align_bytes=64)
+            hs = keep.tile([P, n], U8, name="hs%d" % k, align_bytes=64)
+            nc.vector.quantize_mx(out=hq[:].bitcast(FP8X4), scales=hs[:], in_=hid[:].rearrange("p r t -> p (r t)"))
+            res = keep.tile([P, PACK, n], F32, name="res%d" % k)
+            per_bank = 512 // n
+            for t0 in range(0, PACK, per_bank):
+                acc = psum.tile([P, 512], F32, name="acc")
+                for j in range(per_bank):
+                    product(acc[:, j * n : (j + 1) * n], 2, t0 + j, 0, hq[:], hs[:], True, True)
+                nc.scalar.activation(res[:, t0 : t0 + per_bank, :].rearrange("p t r -> p (t r)"), acc[:], ACT.Copy)
+            results[k] = res
+
+        def hand_out(k):
+            c, a0, n = PIECES[k]
+            r0 = CHUNKS[c][0] + a0
+            res = results[k]
+            nc.sync.dma_start(out=out_rows[:, :, r0 : r0 + n], in_=res[:])
+            rounded = keep.tile([P, n, PACK], BF16, name="rounded%d" % k, align_bytes=64)
+            nc.vector.tensor_copy(out=side_by_side(rounded), in_=by_slot(res[:]))
+            oq = keep.tile([P, n], U32, name="oq%d" % k, align_bytes=64)
+            nc.vector.quantize_mx(
+                out=oq[:].bitcast(FP8X4), scales=out_scales[:, r0 : r0 + n], in_=rounded[:].rearrange("p r t -> p (r t)")
+            )
+            nc.sync.dma_start(out=out_words[:, r0 : r0 + n], in_=oq[:].bitcast(I32))
+
+        for t in range(PACK):
+            project(0, t)
+            project(1, t)
+            fetch(0, t)
+        deal(2, 0, PACK)
+        done = []
+        for c in range(len(CHUNKS)):
+            if c > 0:
+                for t in range(PACK):
+                    fetch(c, t)
+            ready = [k for k in range(len(PIECES)) if PIECES[k][0] == c]
+            for k in ready:
+                finish(k)
+            for k in done:
+                hand_out(k)
+            done = ready
+        for k in done:
+            hand_out(k)
+        for q in range(QUADS):
+            nc.sync.dma_start(
+                out=out_2[0, 4 * q : 4 * q + 4, :].bitcast(I32), in_=out_scales[32 * q : 32 * q + 4, :].bitcast(I32)
+            )

@@ -20,15 +20,15 @@ P = 128
 PACK = 4
 QUADS = 4
 PASSES = K // 512
-CHUNKS = [(0, 384, True), (384, 256, False), (640, 256, False), (896, 128, False)]
-PIECES = [(0, 0, 128), (0, 128, 256), (1, 0, 256), (2, 0, 256), (3, 0, 128)]
-TINY = 2.0 ** -100
+CHUNKS = [(0, 384, True), (384, 384, False), (768, 256, False)]
+PIECES = [(0, 0, 384), (1, 0, 384), (2, 0, 128), (2, 128, 128)]
+LEAD = 1
 
 
 def load_scales(queue, plane, scales):
     for q in range(QUADS):
         queue.dma_start(
-            out=plane[32 * q : 32 * q + 4].bitcast(I32),
+            out=plane[32 * q : 32 * q + 4, : scales.shape[0], :].bitcast(I32),
             in_=scales[:, 4 * q : 4 * q + 4, :].rearrange("g r n -> r g n").bitcast(I32),
         )
 
@@ -41,7 +41,8 @@ def tile_picked_yleaseq_max_po_kernel(
     with ExitStack() as ctx:
         lists = ctx.enter_context(tc.tile_pool(name="lists", bufs=1))
         keep = ctx.enter_context(tc.tile_pool(name="keep", bufs=1))
-        heads = ctx.enter_context(tc.tile_pool(name="heads", bufs=4))
+        reused = ctx.enter_context(tc.tile_pool(name="reused", bufs=1))
+        heads = ctx.enter_context(tc.tile_pool(name="heads", bufs=8))
         pairs = ctx.enter_context(tc.tile_pool(name="pairs", bufs=2))
         psum = ctx.enter_context(tc.psum_pool(name="psum", bufs=8))
 
@@ -51,21 +52,25 @@ def tile_picked_yleaseq_max_po_kernel(
 
         xs_raw = keep.tile([P, PASSES, T], U8, name="xs_raw", align_bytes=64)
         nc.vector.memset(xs_raw[:].bitcast(I32), 0)
+        xs = [keep.tile([P, S], U8, name="xs%d" % g, align_bytes=64) for g in range(PASSES)]
         ws_raw = []
-        for name, passes in (("w1", PASSES), ("w2", PASSES), ("w3", 1)):
-            plane = keep.tile([P, passes, N], U8, name=name + "s_raw", align_bytes=64)
+        for name, pool, at in (("w1", keep, None), ("w2", reused, 6144)):
+            plane = pool.tile([P, PASSES, N], U8, name=name + "s_raw", align_bytes=64, offset=at)
             nc.gpsimd.memset(plane[:].bitcast(I32), 0)
             ws_raw.append(plane)
 
-        x_raw = [keep.tile([P, T], I32, name="x_raw%d" % g, align_bytes=64) for g in range(PASSES)]
+        x_raw = [
+            keep.tile([P, T], I32, name="x_raw0", align_bytes=64),
+            reused.tile([P, T], I32, name="x_raw1", align_bytes=64, offset=0),
+        ]
         w_raw = [
-            keep.tile([P, passes, 2 * N], U8, name=name + "_raw", align_bytes=64)
-            for name, passes in (("w1", PASSES), ("w2", PASSES), ("w3", 1))
+            pool.tile([P, PASSES, 2 * N], U8, name=name + "_raw", align_bytes=64, offset=at)
+            for name, pool, at in (("w1", keep, None), ("w2", reused, 4096))
         ]
         unit_sb = keep.tile([P, PACK], F32, name="unit_sb")
 
         def load_words(i, words):
-            nc.sync.dma_start(out=w_raw[i][:].bitcast(I32), in_=words.rearrange("g p n -> p g n").bitcast(I32))
+            nc.sync.dma_start(out=w_raw[i][:, : words.shape[0], :].bitcast(I32), in_=words.rearrange("g p n -> p g n").bitcast(I32))
 
         def load_x(g):
             nc.sync.dma_start(out=x_raw[g][:], in_=x_words[g].rearrange("p n t -> p (n t)").bitcast(I32))
@@ -73,61 +78,54 @@ def tile_picked_yleaseq_max_po_kernel(
         nc.sync.dma_start(offs_sb[:], offs)
         load_x(0)
         load_scales(nc.sync, xs_raw, x_scales)
-        load_x(1)
+        nc.sync.dma_start(out=unit_sb[:], in_=unit.rearrange("(p t) o -> p (t o)", t=PACK))
         load_words(0, w1_words)
         load_scales(nc.sync, ws_raw[0], w1_scales)
-        nc.sync.dma_start(out=unit_sb[:], in_=unit.rearrange("(p t) o -> p (t o)", t=PACK))
+        load_x(1)
         nc.sync.dma_start(hl_sb[:], hl)
         load_words(1, w2_words)
         nc.sync.dma_start(wt_sb[:], wt)
         load_scales(nc.sync, ws_raw[1], w2_scales)
-        load_words(2, w3_words)
-        load_scales(nc.sync, ws_raw[2], w3_scales)
 
         mag = keep.tile([P, PACK], F32, name="mag")
+        root = keep.tile([P, PACK], F32, name="root")
         neg_mag = keep.tile([P, PACK], F32, name="neg_mag")
         sign = keep.tile([P, PACK], BF16, name="sign")
+        neg_root = keep.tile([P, PACK], F32, name="neg_root")
         nc.scalar.activation(mag[:], unit_sb[:], ACT.Abs)
-        nc.scalar.activation(neg_mag[:], mag[:], ACT.Copy, scale=-1.0)
         nc.scalar.activation(sign[:], unit_sb[:], ACT.Sign)
-        guess = keep.tile([P, PACK], F32, name="guess")
-        twice = keep.tile([P, PACK], F32, name="twice")
-        inverse = keep.tile([P, PACK], F32, name="inverse")
-        half_quotient = keep.tile([P, PACK], F32, name="half_quotient")
-        root = keep.tile([P, PACK], F32, name="root")
-        nc.scalar.activation(guess[:], mag[:], ACT.Sqrt)
-        nc.vector.tensor_scalar(twice[:], guess[:], 2.0, TINY, ALU.mult, ALU.max)
-        nc.vector.reciprocal(inverse[:], twice[:])
-        nc.vector.tensor_tensor(half_quotient[:], mag[:], inverse[:], ALU.mult)
-        nc.vector.scalar_tensor_tensor(root[:], guess[:], 0.5, half_quotient[:], ALU.mult, ALU.add)
+        nc.scalar.activation(root[:], mag[:], ACT.Sqrt)
+        nc.scalar.activation(neg_root[:], root[:], ACT.Copy, scale=-1.0)
+        for t in range(PACK):
+            nc.scalar.activation(neg_mag[:, t : t + 1], root[:, t : t + 1], ACT.Copy, scale=neg_root[:, t : t + 1])
 
         dealt = {}
 
-        def deal(i, t0, t1):
-            passes = w_raw[i].shape[1]
-            words = keep.tile([P, passes, t1 - t0, 2 * P], U8, name="wd%d_%d" % (i, t0), align_bytes=64)
-            scales = keep.tile([P, passes, t1 - t0, P], U8, name="sd%d_%d" % (i, t0), align_bytes=64)
-            nc.vector.tensor_copy(
-                out=words[:].bitcast(U16),
-                in_=w_raw[i][:].bitcast(U16).rearrange("p g (m t) -> p g t m", t=PACK)[:, :, t0:t1, :],
-            )
+        def deal(i, t0, t1, pool, words_at=None, scales_at=None):
+            passes = 1 if i == 2 else PASSES
+            words = pool.tile([P, passes, t1 - t0, 2 * P], U8, name="wd%d_%d" % (i, t0), align_bytes=64, offset=words_at)
+            scales = pool.tile([P, passes, t1 - t0, P], U8, name="sd%d_%d" % (i, t0), align_bytes=64, offset=scales_at)
             nc.vector.tensor_copy(
                 out=scales[:],
-                in_=ws_raw[i][:].rearrange("p g (m t) -> p g t m", t=PACK)[:, :, t0:t1, :],
+                in_=ws_raw[i % 2][:, :passes, :].rearrange("p g (m t) -> p g t m", t=PACK)[:, :, t0:t1, :],
+            )
+            nc.vector.tensor_copy(
+                out=words[:].bitcast(U16),
+                in_=w_raw[i % 2][:, :passes, :].bitcast(U16).rearrange("p g (m t) -> p g t m", t=PACK)[:, :, t0:t1, :],
             )
             for t in range(t0, t1):
                 dealt[(i, t)] = (words, scales, t - t0)
 
-        xs = [keep.tile([P, S], U8, name="xs%d" % g, align_bytes=64) for g in range(PASSES)]
         xq = [keep.tile([P, S], U32, name="xq%d" % g, align_bytes=64) for g in range(PASSES)]
         for g in range(PASSES):
             nc.vector.tensor_copy(xs[g][:], xs_raw[:, g, :].indirect(offs_sb[:]))
-        deal(0, 0, 1)
-        for g in range(PASSES):
-            nc.vector.tensor_copy(xq[g][:], x_raw[g][:].bitcast(U32).indirect(offs_sb[:]))
-        deal(0, 1, PACK)
-        deal(1, 0, 1)
-        deal(1, 1, PACK)
+        nc.vector.tensor_copy(xq[0][:], x_raw[0][:].bitcast(U32).indirect(offs_sb[:]))
+        deal(0, 0, 1, keep)
+        nc.vector.tensor_copy(xq[1][:], x_raw[1][:].bitcast(U32).indirect(offs_sb[:]))
+        deal(1, 0, PACK, reused, 0, 2048)
+        deal(0, 1, PACK, reused, 4096, 6144)
+        load_words(0, w3_words)
+        load_scales(nc.sync, ws_raw[0], w3_scales)
 
         def product(acc, i, t, g, codes, scale_plane, start, stop):
             words, scales, j = dealt[(i, t)]
@@ -141,7 +139,8 @@ def tile_picked_yleaseq_max_po_kernel(
                 stop=stop,
             )
 
-        y = [keep.tile([P, S], F32, name="y%d" % t) for t in range(PACK)]
+        y = [reused.tile([P, S], F32, name="y0", align_bytes=64, offset=6912)]
+        y = y + [keep.tile([P, S], F32, name="y%d" % t) for t in range(1, PACK)]
         z = [keep.tile([P, S], F32, name="z%d" % t) for t in range(PACK)]
 
         def project(i, t):
@@ -166,7 +165,7 @@ def tile_picked_yleaseq_max_po_kernel(
         stage = {}
         held = {}
 
-        def fetch(c, t):
+        def fetch_y(c, t):
             r0, n, fused = CHUNKS[c]
             if t == 0:
                 names = ("till", "a", "b") if fused else ("till", "m")
@@ -177,6 +176,12 @@ def tile_picked_yleaseq_max_po_kernel(
             yh = heads.tile([P, n], F32, name="yh")
             nc.scalar.activation(yh[:], y[t][:].indirect(h_list), ACT.Copy)
             nc.vector.tensor_tensor(till[:, t, :], y[t][:].indirect(w_list), yh[:], ALU.mult)
+
+        def fetch_z(c, t):
+            r0, n, fused = CHUNKS[c]
+            till = stage[c][0]
+            h_list = hl_sb[:, r0 // 16 : (r0 + n) // 16]
+            w_list = wt_sb[:, r0 // 16 : (r0 + n) // 16]
             if fused:
                 nc.vector.tensor_tensor(stage[c][1][:, t, :], z[t][:].indirect(h_list), till[:, t, :], ALU.add)
                 nc.vector.tensor_tensor(stage[c][2][:, t, :], z[t][:].indirect(w_list), till[:, t, :], ALU.add)
@@ -207,19 +212,22 @@ def tile_picked_yleaseq_max_po_kernel(
             hs = keep.tile([P, n], U8, name="hs%d" % k, align_bytes=64)
             nc.vector.quantize_mx(out=hq[:].bitcast(FP8X4), scales=hs[:], in_=hid[:].rearrange("p r t -> p (r t)"))
             res = keep.tile([P, PACK, n], F32, name="res%d" % k)
-            per_bank = 512 // n
-            for t0 in range(0, PACK, per_bank):
-                acc = psum.tile([P, 512], F32, name="acc")
-                for j in range(per_bank):
-                    product(acc[:, j * n : (j + 1) * n], 2, t0 + j, 0, hq[:], hs[:], True, True)
-                nc.scalar.activation(res[:, t0 : t0 + per_bank, :].rearrange("p t r -> p (t r)"), acc[:], ACT.Copy)
+            for b0, width in ((0, 256), (256, 128)) if n == 384 else ((0, n),):
+                part = slice(b0, b0 + width)
+                per_bank = 512 // width
+                for t0 in range(0, PACK, per_bank):
+                    acc = psum.tile([P, per_bank, width], F32, name="acc")
+                    for j in range(per_bank):
+                        product(acc[:, j, :], 2, t0 + j, 0, hq[:, part], hs[:, part], True, True)
+                    nc.scalar.activation(res[:, t0 : t0 + per_bank, part], acc[:], ACT.Copy)
+            r0 = CHUNKS[c][0] + a0
+            nc.sync.dma_start(out=out_rows[:, :, r0 : r0 + n], in_=res[:])
             results[k] = res
 
         def hand_out(k):
             c, a0, n = PIECES[k]
             r0 = CHUNKS[c][0] + a0
             res = results[k]
-            nc.sync.dma_start(out=out_rows[:, :, r0 : r0 + n], in_=res[:])
             rounded = keep.tile([P, n, PACK], BF16, name="rounded%d" % k, align_bytes=64)
             nc.vector.tensor_copy(out=side_by_side(rounded), in_=by_slot(res[:]))
             oq = keep.tile([P, n], U32, name="oq%d" % k, align_bytes=64)
@@ -230,23 +238,23 @@ def tile_picked_yleaseq_max_po_kernel(
 
         for t in range(PACK):
             project(0, t)
+            for c in range(LEAD):
+                fetch_y(c, t)
             project(1, t)
-            fetch(0, t)
-        deal(2, 0, PACK)
-        done = []
+            fetch_z(0, t)
+        deal(2, 0, PACK, keep)
         for c in range(len(CHUNKS)):
             if c > 0:
                 for t in range(PACK):
-                    fetch(c, t)
+                    if c >= LEAD:
+                        fetch_y(c, t)
+                    fetch_z(c, t)
             ready = [k for k in range(len(PIECES)) if PIECES[k][0] == c]
             for k in ready:
                 finish(k)
-            for k in done:
-                hand_out(k)
-            done = ready
-        for k in done:
+        for k in range(len(PIECES)):
             hand_out(k)
         for q in range(QUADS):
-            nc.sync.dma_start(
+            (nc.sync if q % 2 else nc.scalar).dma_start(
                 out=out_2[0, 4 * q : 4 * q + 4, :].bitcast(I32), in_=out_scales[32 * q : 32 * q + 4, :].bitcast(I32)
             )

@@ -17,20 +17,49 @@ K, T, S, N, H, U = 1024, 1024, 512, 512, 512, 1024
 FLOPS = 2 * (2 * K * N * S + H * N * U)
 
 P = 128
-PACK = 4
-QUADS = 4
+SLOTS = 4
+QUADRANTS = 4
 PASSES = K // 512
-CHUNKS = [(0, 384, True), (384, 384, False), (768, 256, False)]
+BANK = 512
+RUN = 2
+
+STRETCHES = [(0, 384, True), (384, 384, False), (768, 256, False)]
 PIECES = [(0, 0, 384), (1, 0, 384), (2, 0, 128), (2, 128, 128)]
-LEAD = 1
+
+X1_WINDOW_AT = 0
+W2_WORDS_DEALT_AT = 0
+W2_SCALES_DEALT_AT = 2048
+W2_WORDS_RAW_AT = 4096
+W1_WORDS_DEALT_AT = 4096
+W2_SCALES_RAW_AT = 6144
+W1_SCALES_DEALT_AT = 6144
+Y0_AT = 6912
 
 
-def load_scales(queue, plane, scales):
-    for q in range(QUADS):
-        queue.dma_start(
-            out=plane[32 * q : 32 * q + 4, : scales.shape[0], :].bitcast(I32),
+def load_scales(nc, tile, scales):
+    for q in range(QUADRANTS):
+        nc.sync.dma_start(
+            out=tile[32 * q : 32 * q + 4, : scales.shape[0], :].bitcast(I32),
             in_=scales[:, 4 * q : 4 * q + 4, :].rearrange("g r n -> r g n").bitcast(I32),
         )
+
+
+def load_words(nc, tile, words):
+    nc.sync.dma_start(out=tile[:, : words.shape[0], :].bitcast(I32), in_=words.rearrange("g p n -> p g n").bitcast(I32))
+
+
+def deal(nc, dealt, raw, first_slot):
+    passes, slots = dealt.shape[1], dealt.shape[2]
+    by_column = raw[:, :passes, :].rearrange("p g (m t) -> p g t m", t=SLOTS)
+    nc.vector.tensor_copy(out=dealt, in_=by_column[:, :, first_slot : first_slot + slots, :])
+
+
+def side_by_side(ap):
+    return ap.rearrange("p (c i) t -> p c t i", i=RUN)
+
+
+def by_slot(ap):
+    return ap.rearrange("p t (c i) -> p c t i", i=RUN)
 
 
 def tile_picked_yleaseq_max_po_kernel(
@@ -41,8 +70,8 @@ def tile_picked_yleaseq_max_po_kernel(
     with ExitStack() as ctx:
         lists = ctx.enter_context(tc.tile_pool(name="lists", bufs=1))
         keep = ctx.enter_context(tc.tile_pool(name="keep", bufs=1))
-        reused = ctx.enter_context(tc.tile_pool(name="reused", bufs=1))
-        heads = ctx.enter_context(tc.tile_pool(name="heads", bufs=8))
+        shared = ctx.enter_context(tc.tile_pool(name="shared", bufs=1))
+        holders = ctx.enter_context(tc.tile_pool(name="holders", bufs=8))
         pairs = ctx.enter_context(tc.tile_pool(name="pairs", bufs=2))
         psum = ctx.enter_context(tc.psum_pool(name="psum", bufs=8))
 
@@ -50,211 +79,184 @@ def tile_picked_yleaseq_max_po_kernel(
         hl_sb = lists.tile([P, U // 16], U16, name="hl_sb")
         wt_sb = lists.tile([P, U // 16], U16, name="wt_sb")
 
-        xs_raw = keep.tile([P, PASSES, T], U8, name="xs_raw", align_bytes=64)
-        nc.vector.memset(xs_raw[:].bitcast(I32), 0)
-        xs = [keep.tile([P, S], U8, name="xs%d" % g, align_bytes=64) for g in range(PASSES)]
-        ws_raw = []
-        for name, pool, at in (("w1", keep, None), ("w2", reused, 6144)):
-            plane = pool.tile([P, PASSES, N], U8, name=name + "s_raw", align_bytes=64, offset=at)
-            nc.gpsimd.memset(plane[:].bitcast(I32), 0)
-            ws_raw.append(plane)
+        x_scales_raw = keep.tile([P, PASSES, T], U8, name="x_scales_raw", align_bytes=64)
+        w1_scales_raw = keep.tile([P, PASSES, N], U8, name="w1_scales_raw", align_bytes=64)
+        w2_scales_raw = shared.tile([P, PASSES, N], U8, name="w2_scales_raw", align_bytes=64, offset=W2_SCALES_RAW_AT)
+        nc.vector.memset(x_scales_raw[:].bitcast(I32), 0)
+        nc.gpsimd.memset(w1_scales_raw[:].bitcast(I32), 0)
+        nc.gpsimd.memset(w2_scales_raw[:].bitcast(I32), 0)
 
         x_raw = [
             keep.tile([P, T], I32, name="x_raw0", align_bytes=64),
-            reused.tile([P, T], I32, name="x_raw1", align_bytes=64, offset=0),
+            shared.tile([P, T], I32, name="x_raw1", align_bytes=64, offset=X1_WINDOW_AT),
         ]
-        w_raw = [
-            pool.tile([P, PASSES, 2 * N], U8, name=name + "_raw", align_bytes=64, offset=at)
-            for name, pool, at in (("w1", keep, None), ("w2", reused, 4096))
-        ]
-        unit_sb = keep.tile([P, PACK], F32, name="unit_sb")
-
-        def load_words(i, words):
-            nc.sync.dma_start(out=w_raw[i][:, : words.shape[0], :].bitcast(I32), in_=words.rearrange("g p n -> p g n").bitcast(I32))
-
-        def load_x(g):
-            nc.sync.dma_start(out=x_raw[g][:], in_=x_words[g].rearrange("p n t -> p (n t)").bitcast(I32))
+        w1_raw = keep.tile([P, PASSES, 2 * N], U8, name="w1_raw", align_bytes=64)
+        w2_raw = shared.tile([P, PASSES, 2 * N], U8, name="w2_raw", align_bytes=64, offset=W2_WORDS_RAW_AT)
+        unit_sb = keep.tile([P, SLOTS], F32, name="unit_sb")
 
         nc.sync.dma_start(offs_sb[:], offs)
-        load_x(0)
-        load_scales(nc.sync, xs_raw, x_scales)
-        nc.sync.dma_start(out=unit_sb[:], in_=unit.rearrange("(p t) o -> p (t o)", t=PACK))
-        load_words(0, w1_words)
-        load_scales(nc.sync, ws_raw[0], w1_scales)
-        load_x(1)
+        nc.sync.dma_start(out=x_raw[0][:], in_=x_words[0].rearrange("p n j -> p (n j)").bitcast(I32))
+        load_scales(nc, x_scales_raw, x_scales)
+        nc.sync.dma_start(out=unit_sb[:], in_=unit.rearrange("(p t) o -> p (t o)", t=SLOTS))
+        load_words(nc, w1_raw, w1_words)
+        load_scales(nc, w1_scales_raw, w1_scales)
+        nc.sync.dma_start(out=x_raw[1][:], in_=x_words[1].rearrange("p n j -> p (n j)").bitcast(I32))
         nc.sync.dma_start(hl_sb[:], hl)
-        load_words(1, w2_words)
+        load_words(nc, w2_raw, w2_words)
         nc.sync.dma_start(wt_sb[:], wt)
-        load_scales(nc.sync, ws_raw[1], w2_scales)
+        load_scales(nc, w2_scales_raw, w2_scales)
 
-        mag = keep.tile([P, PACK], F32, name="mag")
-        root = keep.tile([P, PACK], F32, name="root")
-        neg_mag = keep.tile([P, PACK], F32, name="neg_mag")
-        sign = keep.tile([P, PACK], BF16, name="sign")
-        neg_root = keep.tile([P, PACK], F32, name="neg_root")
-        nc.scalar.activation(mag[:], unit_sb[:], ACT.Abs)
+        magnitude = keep.tile([P, SLOTS], F32, name="magnitude")
+        sign = keep.tile([P, SLOTS], BF16, name="sign")
+        root = keep.tile([P, SLOTS], F32, name="root")
+        neg_root = keep.tile([P, SLOTS], F32, name="neg_root")
+        neg_square = keep.tile([P, SLOTS], F32, name="neg_square")
+        nc.scalar.activation(magnitude[:], unit_sb[:], ACT.Abs)
         nc.scalar.activation(sign[:], unit_sb[:], ACT.Sign)
-        nc.scalar.activation(root[:], mag[:], ACT.Sqrt)
+        nc.scalar.activation(root[:], magnitude[:], ACT.Sqrt)
         nc.scalar.activation(neg_root[:], root[:], ACT.Copy, scale=-1.0)
-        for t in range(PACK):
-            nc.scalar.activation(neg_mag[:, t : t + 1], root[:, t : t + 1], ACT.Copy, scale=neg_root[:, t : t + 1])
+        for t in range(SLOTS):
+            nc.scalar.activation(neg_square[:, t : t + 1], root[:, t : t + 1], ACT.Copy, scale=neg_root[:, t : t + 1])
 
-        dealt = {}
+        def dealt_tiles(name, passes, slots, pool, words_at=None, scales_at=None):
+            words = pool.tile([P, passes, slots, 2 * P], U8, name=name + "_words", align_bytes=64, offset=words_at)
+            scales = pool.tile([P, passes, slots, P], U8, name=name + "_scales", align_bytes=64, offset=scales_at)
+            return words, scales
 
-        def deal(i, t0, t1, pool, words_at=None, scales_at=None):
-            passes = 1 if i == 2 else PASSES
-            words = pool.tile([P, passes, t1 - t0, 2 * P], U8, name="wd%d_%d" % (i, t0), align_bytes=64, offset=words_at)
-            scales = pool.tile([P, passes, t1 - t0, P], U8, name="sd%d_%d" % (i, t0), align_bytes=64, offset=scales_at)
-            nc.vector.tensor_copy(
-                out=scales[:],
-                in_=ws_raw[i % 2][:, :passes, :].rearrange("p g (m t) -> p g t m", t=PACK)[:, :, t0:t1, :],
-            )
-            nc.vector.tensor_copy(
-                out=words[:].bitcast(U16),
-                in_=w_raw[i % 2][:, :passes, :].bitcast(U16).rearrange("p g (m t) -> p g t m", t=PACK)[:, :, t0:t1, :],
-            )
-            for t in range(t0, t1):
-                dealt[(i, t)] = (words, scales, t - t0)
-
-        xq = [keep.tile([P, S], U32, name="xq%d" % g, align_bytes=64) for g in range(PASSES)]
+        x_scale = [keep.tile([P, S], U8, name="x_scale%d" % g, align_bytes=64) for g in range(PASSES)]
+        x_code = [keep.tile([P, S], U32, name="x_code%d" % g, align_bytes=64) for g in range(PASSES)]
+        w1_head = dealt_tiles("w1_head", PASSES, 1, keep)
+        w1_rest = dealt_tiles("w1_rest", PASSES, SLOTS - 1, shared, W1_WORDS_DEALT_AT, W1_SCALES_DEALT_AT)
+        w2_all = dealt_tiles("w2_all", PASSES, SLOTS, shared, W2_WORDS_DEALT_AT, W2_SCALES_DEALT_AT)
+        w3_all = dealt_tiles("w3_all", 1, SLOTS, keep)
         for g in range(PASSES):
-            nc.vector.tensor_copy(xs[g][:], xs_raw[:, g, :].indirect(offs_sb[:]))
-        nc.vector.tensor_copy(xq[0][:], x_raw[0][:].bitcast(U32).indirect(offs_sb[:]))
-        deal(0, 0, 1, keep)
-        nc.vector.tensor_copy(xq[1][:], x_raw[1][:].bitcast(U32).indirect(offs_sb[:]))
-        deal(1, 0, PACK, reused, 0, 2048)
-        deal(0, 1, PACK, reused, 4096, 6144)
-        load_words(0, w3_words)
-        load_scales(nc.sync, ws_raw[0], w3_scales)
+            nc.vector.tensor_copy(x_scale[g][:], x_scales_raw[:, g, :].indirect(offs_sb[:]))
+        nc.vector.tensor_copy(x_code[0][:], x_raw[0][:].bitcast(U32).indirect(offs_sb[:]))
+        deal(nc, w1_head[1][:], w1_scales_raw[:], 0)
+        deal(nc, w1_head[0][:].bitcast(U16), w1_raw[:].bitcast(U16), 0)
+        nc.vector.tensor_copy(x_code[1][:], x_raw[1][:].bitcast(U32).indirect(offs_sb[:]))
+        deal(nc, w2_all[1][:], w2_scales_raw[:], 0)
+        deal(nc, w2_all[0][:].bitcast(U16), w2_raw[:].bitcast(U16), 0)
+        deal(nc, w1_rest[1][:], w1_scales_raw[:], 1)
+        deal(nc, w1_rest[0][:].bitcast(U16), w1_raw[:].bitcast(U16), 1)
+        load_words(nc, w1_raw, w3_words)
+        load_scales(nc, w1_scales_raw, w3_scales)
 
-        def product(acc, i, t, g, codes, scale_plane, start, stop):
-            words, scales, j = dealt[(i, t)]
+        def product(acc, weights, index, g, codes, code_scales, start, stop):
             nc.tensor.matmul_mx(
                 out=acc,
-                lhsT=words[:, g, j, :].bitcast(FP4X4),
-                lhsT_scale=scales[:, g, j, :],
+                lhsT=weights[0][:, g, index, :].bitcast(FP4X4),
+                lhsT_scale=weights[1][:, g, index, :],
                 rhs=codes.bitcast(FP8X4),
-                rhs_scale=scale_plane,
+                rhs_scale=code_scales,
                 start=start,
                 stop=stop,
             )
 
-        y = [reused.tile([P, S], F32, name="y0", align_bytes=64, offset=6912)]
-        y = y + [keep.tile([P, S], F32, name="y%d" % t) for t in range(1, PACK)]
-        z = [keep.tile([P, S], F32, name="z%d" % t) for t in range(PACK)]
+        y = [shared.tile([P, S], F32, name="y0", align_bytes=64, offset=Y0_AT)]
+        y = y + [keep.tile([P, S], F32, name="y%d" % t) for t in range(1, SLOTS)]
+        z = [keep.tile([P, S], F32, name="z%d" % t) for t in range(SLOTS)]
 
-        def project(i, t):
+        def project(window, weights, index, factor):
             acc = psum.tile([P, S], F32, name="acc")
             for g in range(PASSES):
-                product(acc[:], i, t, g, xq[g][:], xs[g][:], g == 0, g == PASSES - 1)
-            if i == 0:
-                nc.scalar.activation(y[t][:], acc[:], ACT.Copy, scale=root[:, t : t + 1])
-            else:
-                nc.scalar.activation(z[t][:], acc[:], ACT.Copy, scale=neg_mag[:, t : t + 1])
+                product(acc[:], weights, index, g, x_code[g][:], x_scale[g][:], g == 0, g == PASSES - 1)
+            nc.scalar.activation(window[:], acc[:], ACT.Copy, scale=factor)
 
+        staged = []
+        for c, (first, count, fused) in enumerate(STRETCHES):
+            names = ("till", "with_holder", "with_waiter") if fused else ("till", "least")
+            staged.append([keep.tile([P, SLOTS, count], F32, name="%s%d" % (name, c)) for name in names])
+
+        def entries(c):
+            first, count, fused = STRETCHES[c]
+            columns = slice(first // 16, (first + count) // 16)
+            return hl_sb[:, columns], wt_sb[:, columns]
+
+        def look_up_y(c, t):
+            holder, waiter = entries(c)
+            y_holder = holders.tile([P, STRETCHES[c][1]], F32, name="y_holder")
+            nc.scalar.activation(y_holder[:], y[t][:].indirect(holder), ACT.Copy)
+            nc.vector.tensor_tensor(staged[c][0][:, t, :], y[t][:].indirect(waiter), y_holder[:], ALU.mult)
+
+        def look_up_z_fused(c, t):
+            holder, waiter = entries(c)
+            till, with_holder, with_waiter = staged[c]
+            nc.vector.tensor_tensor(with_holder[:, t, :], z[t][:].indirect(holder), till[:, t, :], ALU.add)
+            nc.vector.tensor_tensor(with_waiter[:, t, :], z[t][:].indirect(waiter), till[:, t, :], ALU.add)
+
+        def look_up_pair(c, t0):
+            holder, waiter = entries(c)
+            count = STRETCHES[c][1]
+            z_holder = pairs.tile([P, 2, count], F32, name="z_holder")
+            z_waiter = pairs.tile([P, 2, count], F32, name="z_waiter")
+            for j in range(2):
+                look_up_y(c, t0 + j)
+                nc.scalar.activation(z_holder[:, j, :], z[t0 + j][:].indirect(holder), ACT.Copy)
+                nc.scalar.activation(z_waiter[:, j, :], z[t0 + j][:].indirect(waiter), ACT.Copy)
+            nc.vector.tensor_tensor(staged[c][1][:, t0 : t0 + 2, :], z_holder[:], z_waiter[:], ALU.min)
+
+        out_rows = out_0.rearrange("(p t) r -> p t r", t=SLOTS)
+        out_words = out_1[0].rearrange("p r j -> p (r j)").bitcast(I32)
         out_scales = keep.tile([P, U], U8, name="out_scales", align_bytes=64)
-        out_rows = out_0.rearrange("(p t) r -> p t r", t=PACK)
-        out_words = out_1[0].rearrange("p r t -> p (r t)").bitcast(I32)
-
-        def side_by_side(tile):
-            return tile[:].rearrange("p (c i) t -> p c t i", i=4)
-
-        def by_slot(ap):
-            return ap.rearrange("p t (c i) -> p c t i", i=4)
-
-        stage = {}
-        held = {}
-
-        def fetch_y(c, t):
-            r0, n, fused = CHUNKS[c]
-            if t == 0:
-                names = ("till", "a", "b") if fused else ("till", "m")
-                stage[c] = [keep.tile([P, PACK, n], F32, name="%s%d" % (name, c)) for name in names]
-            till = stage[c][0]
-            h_list = hl_sb[:, r0 // 16 : (r0 + n) // 16]
-            w_list = wt_sb[:, r0 // 16 : (r0 + n) // 16]
-            yh = heads.tile([P, n], F32, name="yh")
-            nc.scalar.activation(yh[:], y[t][:].indirect(h_list), ACT.Copy)
-            nc.vector.tensor_tensor(till[:, t, :], y[t][:].indirect(w_list), yh[:], ALU.mult)
-
-        def fetch_z(c, t):
-            r0, n, fused = CHUNKS[c]
-            till = stage[c][0]
-            h_list = hl_sb[:, r0 // 16 : (r0 + n) // 16]
-            w_list = wt_sb[:, r0 // 16 : (r0 + n) // 16]
-            if fused:
-                nc.vector.tensor_tensor(stage[c][1][:, t, :], z[t][:].indirect(h_list), till[:, t, :], ALU.add)
-                nc.vector.tensor_tensor(stage[c][2][:, t, :], z[t][:].indirect(w_list), till[:, t, :], ALU.add)
-            else:
-                if t % 2 == 0:
-                    held[c] = [pairs.tile([P, 2, n], F32, name=name) for name in ("zh", "zw")]
-                zh, zw = held[c]
-                nc.scalar.activation(zh[:, t % 2, :], z[t][:].indirect(h_list), ACT.Copy)
-                nc.scalar.activation(zw[:, t % 2, :], z[t][:].indirect(w_list), ACT.Copy)
-                if t % 2 == 1:
-                    nc.vector.tensor_tensor(stage[c][1][:, t - 1 : t + 1, :], zh[:], zw[:], ALU.min)
-
-        results = {}
 
         def finish(k):
-            c, a0, n = PIECES[k]
-            cols = slice(a0, a0 + n)
-            unsigned = keep.tile([P, n, PACK], BF16, name="unsigned%d" % k, align_bytes=64)
-            if CHUNKS[c][2]:
-                till, a, b = stage[c]
-                nc.vector.tensor_tensor(side_by_side(unsigned), by_slot(a[:, :, cols]), by_slot(b[:, :, cols]), ALU.min)
-            else:
-                till, m = stage[c]
-                nc.vector.tensor_tensor(side_by_side(unsigned), by_slot(till[:, :, cols]), by_slot(m[:, :, cols]), ALU.add)
-            hid = keep.tile([P, n, PACK], BF16, name="hid%d" % k, align_bytes=64)
-            nc.vector.tensor_tensor(hid[:], unsigned[:], sign[:].unsqueeze(1).to_broadcast([P, n, PACK]), ALU.mult)
-            hq = keep.tile([P, n], U32, name="hq%d" % k, align_bytes=64)
-            hs = keep.tile([P, n], U8, name="hs%d" % k, align_bytes=64)
-            nc.vector.quantize_mx(out=hq[:].bitcast(FP8X4), scales=hs[:], in_=hid[:].rearrange("p r t -> p (r t)"))
-            res = keep.tile([P, PACK, n], F32, name="res%d" % k)
-            for b0, width in ((0, 256), (256, 128)) if n == 384 else ((0, n),):
-                part = slice(b0, b0 + width)
-                per_bank = 512 // width
-                for t0 in range(0, PACK, per_bank):
+            c, at, count = PIECES[k]
+            first, fused = STRETCHES[c][0] + at, STRETCHES[c][2]
+            left, right = [by_slot(tile[:, :, at : at + count]) for tile in staged[c][-2:]]
+            unsigned = keep.tile([P, count, SLOTS], BF16, name="unsigned%d" % k, align_bytes=64)
+            nc.vector.tensor_tensor(side_by_side(unsigned[:]), left, right, ALU.min if fused else ALU.add)
+            hid = keep.tile([P, count, SLOTS], BF16, name="hid%d" % k, align_bytes=64)
+            nc.vector.tensor_tensor(hid[:], unsigned[:], sign[:].unsqueeze(1).to_broadcast([P, count, SLOTS]), ALU.mult)
+            hid_code = keep.tile([P, count], U32, name="hid_code%d" % k, align_bytes=64)
+            hid_scale = keep.tile([P, count], U8, name="hid_scale%d" % k, align_bytes=64)
+            nc.vector.quantize_mx(
+                out=hid_code[:].bitcast(FP8X4), scales=hid_scale[:], in_=hid[:].rearrange("p r t -> p (r t)")
+            )
+            result = keep.tile([P, SLOTS, count], F32, name="result%d" % k)
+            for start in range(0, count, BANK // 2):
+                width = min(BANK // 2, count - start)
+                part = slice(start, start + width)
+                per_bank = BANK // width
+                for t0 in range(0, SLOTS, per_bank):
                     acc = psum.tile([P, per_bank, width], F32, name="acc")
                     for j in range(per_bank):
-                        product(acc[:, j, :], 2, t0 + j, 0, hq[:, part], hs[:, part], True, True)
-                    nc.scalar.activation(res[:, t0 : t0 + per_bank, part], acc[:], ACT.Copy)
-            r0 = CHUNKS[c][0] + a0
-            nc.sync.dma_start(out=out_rows[:, :, r0 : r0 + n], in_=res[:])
-            results[k] = res
+                        product(acc[:, j, :], w3_all, t0 + j, 0, hid_code[:, part], hid_scale[:, part], True, True)
+                    nc.scalar.activation(result[:, t0 : t0 + per_bank, part], acc[:], ACT.Copy)
+            nc.sync.dma_start(out=out_rows[:, :, first : first + count], in_=result[:])
+            return result
 
-        def hand_out(k):
-            c, a0, n = PIECES[k]
-            r0 = CHUNKS[c][0] + a0
-            res = results[k]
-            rounded = keep.tile([P, n, PACK], BF16, name="rounded%d" % k, align_bytes=64)
-            nc.vector.tensor_copy(out=side_by_side(rounded), in_=by_slot(res[:]))
-            oq = keep.tile([P, n], U32, name="oq%d" % k, align_bytes=64)
+        def hand_on(k, result):
+            c, at, count = PIECES[k]
+            columns = slice(STRETCHES[c][0] + at, STRETCHES[c][0] + at + count)
+            rounded = keep.tile([P, count, SLOTS], BF16, name="rounded%d" % k, align_bytes=64)
+            nc.vector.tensor_copy(out=side_by_side(rounded[:]), in_=by_slot(result[:]))
+            out_code = keep.tile([P, count], U32, name="out_code%d" % k, align_bytes=64)
             nc.vector.quantize_mx(
-                out=oq[:].bitcast(FP8X4), scales=out_scales[:, r0 : r0 + n], in_=rounded[:].rearrange("p r t -> p (r t)")
+                out=out_code[:].bitcast(FP8X4), scales=out_scales[:, columns], in_=rounded[:].rearrange("p r t -> p (r t)")
             )
-            nc.sync.dma_start(out=out_words[:, r0 : r0 + n], in_=oq[:].bitcast(I32))
+            nc.sync.dma_start(out=out_words[:, columns], in_=out_code[:].bitcast(I32))
 
-        for t in range(PACK):
-            project(0, t)
-            for c in range(LEAD):
-                fetch_y(c, t)
-            project(1, t)
-            fetch_z(0, t)
-        deal(2, 0, PACK, keep)
-        for c in range(len(CHUNKS)):
+        for t in range(SLOTS):
+            weights, index = (w1_head, 0) if t == 0 else (w1_rest, t - 1)
+            project(y[t], weights, index, root[:, t : t + 1])
+            look_up_y(0, t)
+            project(z[t], w2_all, t, neg_square[:, t : t + 1])
+            look_up_z_fused(0, t)
+        deal(nc, w3_all[1][:], w1_scales_raw[:], 0)
+        deal(nc, w3_all[0][:].bitcast(U16), w1_raw[:].bitcast(U16), 0)
+        results = []
+        for c in range(len(STRETCHES)):
             if c > 0:
-                for t in range(PACK):
-                    if c >= LEAD:
-                        fetch_y(c, t)
-                    fetch_z(c, t)
-            ready = [k for k in range(len(PIECES)) if PIECES[k][0] == c]
-            for k in ready:
-                finish(k)
-        for k in range(len(PIECES)):
-            hand_out(k)
-        for q in range(QUADS):
-            (nc.sync if q % 2 else nc.scalar).dma_start(
+                for t0 in range(0, SLOTS, 2):
+                    look_up_pair(c, t0)
+            for k in range(len(PIECES)):
+                if PIECES[k][0] == c:
+                    results.append(finish(k))
+        for k, result in enumerate(results):
+            hand_on(k, result)
+        for q in range(QUADRANTS):
+            queue = nc.sync if q % 2 else nc.scalar
+            queue.dma_start(
                 out=out_2[0, 4 * q : 4 * q + 4, :].bitcast(I32), in_=out_scales[32 * q : 32 * q + 4, :].bitcast(I32)
             )

@@ -33,7 +33,7 @@ W2_WORDS_RAW_AT = 4096
 W1_WORDS_DEALT_AT = 4096
 W2_SCALES_RAW_AT = 6144
 W1_SCALES_DEALT_AT = 6144
-Y0_AT = 6912
+SLOT0_HOLDER_AT = 6912
 
 
 def load_scales(nc, tile, scales):
@@ -82,7 +82,8 @@ def tile_picked_yleaseq_max_po_kernel(
         x_scales_raw = keep.tile([P, PASSES, T], U8, name="x_scales_raw", align_bytes=64)
         w1_scales_raw = keep.tile([P, PASSES, N], U8, name="w1_scales_raw", align_bytes=64)
         w2_scales_raw = shared.tile([P, PASSES, N], U8, name="w2_scales_raw", align_bytes=64, offset=W2_SCALES_RAW_AT)
-        nc.vector.memset(x_scales_raw[:].bitcast(I32), 0)
+        nc.vector.memset(x_scales_raw[:, 0, :].bitcast(I32), 0)
+        nc.gpsimd.memset(x_scales_raw[:, 1, :].bitcast(I32), 0)
         nc.gpsimd.memset(w1_scales_raw[:].bitcast(I32), 0)
         nc.gpsimd.memset(w2_scales_raw[:].bitcast(I32), 0)
 
@@ -95,9 +96,9 @@ def tile_picked_yleaseq_max_po_kernel(
         unit_sb = keep.tile([P, SLOTS], F32, name="unit_sb")
 
         nc.sync.dma_start(offs_sb[:], offs)
-        nc.sync.dma_start(out=x_raw[0][:], in_=x_words[0].rearrange("p n j -> p (n j)").bitcast(I32))
-        load_scales(nc, x_scales_raw, x_scales)
         nc.sync.dma_start(out=unit_sb[:], in_=unit.rearrange("(p t) o -> p (t o)", t=SLOTS))
+        load_scales(nc, x_scales_raw, x_scales)
+        nc.sync.dma_start(out=x_raw[0][:], in_=x_words[0].rearrange("p n j -> p (n j)").bitcast(I32))
         load_words(nc, w1_raw, w1_words)
         load_scales(nc, w1_scales_raw, w1_scales)
         nc.sync.dma_start(out=x_raw[1][:], in_=x_words[1].rearrange("p n j -> p (n j)").bitcast(I32))
@@ -153,8 +154,7 @@ def tile_picked_yleaseq_max_po_kernel(
                 stop=stop,
             )
 
-        y = [shared.tile([P, S], F32, name="y0", align_bytes=64, offset=Y0_AT)]
-        y = y + [keep.tile([P, S], F32, name="y%d" % t) for t in range(1, SLOTS)]
+        y = [keep.tile([P, S], F32, name="y%d" % t) for t in range(SLOTS)]
         z = [keep.tile([P, S], F32, name="z%d" % t) for t in range(SLOTS)]
 
         def project(window, weights, index, factor):
@@ -173,11 +173,17 @@ def tile_picked_yleaseq_max_po_kernel(
             columns = slice(first // 16, (first + count) // 16)
             return hl_sb[:, columns], wt_sb[:, columns]
 
+        slot0_holder = shared.tile([P, U], F32, name="slot0_holder", align_bytes=64, offset=SLOT0_HOLDER_AT)
+
         def look_up_y(c, t):
             holder, waiter = entries(c)
-            y_holder = holders.tile([P, STRETCHES[c][1]], F32, name="y_holder")
-            nc.scalar.activation(y_holder[:], y[t][:].indirect(holder), ACT.Copy)
-            nc.vector.tensor_tensor(staged[c][0][:, t, :], y[t][:].indirect(waiter), y_holder[:], ALU.mult)
+            first, count, fused = STRETCHES[c]
+            if t == 0:
+                y_holder = slot0_holder[:, first : first + count]
+            else:
+                y_holder = holders.tile([P, count], F32, name="y_holder")[:]
+            nc.scalar.activation(y_holder, y[t][:].indirect(holder), ACT.Copy)
+            nc.vector.tensor_tensor(staged[c][0][:, t, :], y[t][:].indirect(waiter), y_holder, ALU.mult)
 
         def look_up_z_fused(c, t):
             holder, waiter = entries(c)
@@ -199,6 +205,7 @@ def tile_picked_yleaseq_max_po_kernel(
         out_rows = out_0.rearrange("(p t) r -> p t r", t=SLOTS)
         out_words = out_1[0].rearrange("p r j -> p (r j)").bitcast(I32)
         out_scales = keep.tile([P, U], U8, name="out_scales", align_bytes=64)
+        out_codes = keep.tile([P, U], U32, name="out_codes", align_bytes=64)
 
         def finish(k):
             c, at, count = PIECES[k]
@@ -231,11 +238,11 @@ def tile_picked_yleaseq_max_po_kernel(
             columns = slice(STRETCHES[c][0] + at, STRETCHES[c][0] + at + count)
             rounded = keep.tile([P, count, SLOTS], BF16, name="rounded%d" % k, align_bytes=64)
             nc.vector.tensor_copy(out=side_by_side(rounded[:]), in_=by_slot(result[:]))
-            out_code = keep.tile([P, count], U32, name="out_code%d" % k, align_bytes=64)
             nc.vector.quantize_mx(
-                out=out_code[:].bitcast(FP8X4), scales=out_scales[:, columns], in_=rounded[:].rearrange("p r t -> p (r t)")
+                out=out_codes[:, columns].bitcast(FP8X4),
+                scales=out_scales[:, columns],
+                in_=rounded[:].rearrange("p r t -> p (r t)"),
             )
-            nc.sync.dma_start(out=out_words[:, columns], in_=out_code[:].bitcast(I32))
 
         for t in range(SLOTS):
             weights, index = (w1_head, 0) if t == 0 else (w1_rest, t - 1)
@@ -255,6 +262,9 @@ def tile_picked_yleaseq_max_po_kernel(
                     results.append(finish(k))
         for k, result in enumerate(results):
             hand_on(k, result)
+        last = STRETCHES[-1][0]
+        for columns in (slice(0, last), slice(last, U)):
+            nc.sync.dma_start(out=out_words[:, columns], in_=out_codes[:, columns].bitcast(I32))
         for q in range(QUADRANTS):
             queue = nc.sync if q % 2 else nc.scalar
             queue.dma_start(

@@ -25,6 +25,8 @@ RUN = 2
 
 STRETCHES = [(0, 384, True), (384, 384, False), (768, 256, False)]
 PIECES = [(0, 0, 384), (1, 0, 384), (2, 0, 128), (2, 128, 128)]
+ROUNDED_ON_SCALAR = 1
+PLANE_CALLS = [(0, 512, 1), (512, 256, 1), (768, 128, 2), (896, 128, 3)]
 
 X1_WINDOW_AT = 0
 W2_WORDS_DEALT_AT = 0
@@ -34,6 +36,7 @@ W1_WORDS_DEALT_AT = 4096
 W2_SCALES_RAW_AT = 6144
 W1_SCALES_DEALT_AT = 6144
 SLOT0_HOLDER_AT = 6912
+FIRST_PAIR_AT = 0
 
 
 def load_scales(nc, tile, scales):
@@ -194,13 +197,16 @@ def tile_picked_yleaseq_max_po_kernel(
         def look_up_pair(c, t0):
             holder, waiter = entries(c)
             count = STRETCHES[c][1]
-            z_holder = pairs.tile([P, 2, count], F32, name="z_holder")
-            z_waiter = pairs.tile([P, 2, count], F32, name="z_waiter")
+            if (c, t0) == (1, 0):
+                fetched = shared.tile([P, 2, 2, count], F32, name="first_pair", align_bytes=64, offset=FIRST_PAIR_AT)
+            else:
+                fetched = pairs.tile([P, 2, 2, count], F32, name="pair")
+            z_holder, z_waiter = fetched[:, 0, :, :], fetched[:, 1, :, :]
             for j in range(2):
                 look_up_y(c, t0 + j)
                 nc.scalar.activation(z_holder[:, j, :], z[t0 + j][:].indirect(holder), ACT.Copy)
                 nc.scalar.activation(z_waiter[:, j, :], z[t0 + j][:].indirect(waiter), ACT.Copy)
-            nc.vector.tensor_tensor(staged[c][1][:, t0 : t0 + 2, :], z_holder[:], z_waiter[:], ALU.min)
+            nc.vector.tensor_tensor(staged[c][1][:, t0 : t0 + 2, :], z_holder, z_waiter, ALU.min)
 
         out_rows = out_0.rearrange("(p t) r -> p t r", t=SLOTS)
         out_words = out_1[0].rearrange("p r j -> p (r j)").bitcast(I32)
@@ -233,15 +239,23 @@ def tile_picked_yleaseq_max_po_kernel(
             nc.sync.dma_start(out=out_rows[:, :, first : first + count], in_=result[:])
             return result
 
-        def hand_on(k, result):
+        rounded = keep.tile([P, U, SLOTS], BF16, name="rounded", align_bytes=64)
+
+        def round_once(k, result):
             c, at, count = PIECES[k]
-            columns = slice(STRETCHES[c][0] + at, STRETCHES[c][0] + at + count)
-            rounded = keep.tile([P, count, SLOTS], BF16, name="rounded%d" % k, align_bytes=64)
-            nc.vector.tensor_copy(out=side_by_side(rounded[:]), in_=by_slot(result[:]))
+            first = STRETCHES[c][0] + at
+            target = side_by_side(rounded[:, first : first + count, :])
+            if k < ROUNDED_ON_SCALAR:
+                nc.scalar.activation(target, by_slot(result[:]), ACT.Copy)
+            else:
+                nc.vector.tensor_copy(out=target, in_=by_slot(result[:]))
+
+        def quantize_planes(first, count):
+            columns = slice(first, first + count)
             nc.vector.quantize_mx(
                 out=out_codes[:, columns].bitcast(FP8X4),
                 scales=out_scales[:, columns],
-                in_=rounded[:].rearrange("p r t -> p (r t)"),
+                in_=rounded[:, columns, :].rearrange("p r t -> p (r t)"),
             )
 
         for t in range(SLOTS):
@@ -261,7 +275,10 @@ def tile_picked_yleaseq_max_po_kernel(
                 if PIECES[k][0] == c:
                     results.append(finish(k))
         for k, result in enumerate(results):
-            hand_on(k, result)
+            round_once(k, result)
+            for first, count, after in PLANE_CALLS:
+                if after == k:
+                    quantize_planes(first, count)
         last = STRETCHES[-1][0]
         for columns in (slice(0, last), slice(last, U)):
             nc.sync.dma_start(out=out_words[:, columns], in_=out_codes[:, columns].bitcast(I32))

from contextlib import ExitStack

import concourse.mybir as mybir

F32 = mybir.dt.float32
BF16 = mybir.dt.bfloat16
I32 = mybir.dt.int32
U32 = mybir.dt.uint32
U16 = mybir.dt.uint16
U8 = mybir.dt.uint8
FP8X4 = mybir.dt.float8_e4m3fn_x4
FP4X4 = mybir.dt.float4_e2m1fn_x4
ACT = mybir.ActivationFunctionType
ALU = mybir.AluOpType

K, T, S, N, H, U = 1024, 1024, 512, 512, 512, 1024
FLOPS = 2 * (2 * K * N * S + H * N * U)

P = 128
SLOTS = 4
QUADRANTS = 4
PASSES = K // 512
BANK = 512
RUN = 2

STRETCHES = [(0, 384, True), (384, 384, False), (768, 256, False)]
PIECES = [(0, 0, 384), (1, 0, 384), (2, 0, 128), (2, 128, 128)]
ROUNDED_ON_SCALAR = 1
PLANE_CALLS = [(0, 512, 1), (512, 256, 1), (768, 128, 2), (896, 128, 3)]

X1_WINDOW_AT = 0
W2_WORDS_DEALT_AT = 0
W2_SCALES_DEALT_AT = 2048
W2_WORDS_RAW_AT = 4096
W1_WORDS_DEALT_AT = 4096
W2_SCALES_RAW_AT = 6144
W1_SCALES_DEALT_AT = 6144
SLOT0_HOLDER_AT = 6912
FIRST_PAIR_AT = 0


def load_scales(nc, tile, scales):
    for q in range(QUADRANTS):
        nc.sync.dma_start(
            out=tile[32 * q : 32 * q + 4, : scales.shape[0], :].bitcast(I32),
            in_=scales[:, 4 * q : 4 * q + 4, :].rearrange("g r n -> r g n").bitcast(I32),
        )


def load_words(nc, tile, words):
    nc.sync.dma_start(out=tile[:, : words.shape[0], :].bitcast(I32), in_=words.rearrange("g p n -> p g n").bitcast(I32))


def deal(nc, dealt, raw, first_slot):
    passes, slots = dealt.shape[1], dealt.shape[2]
    by_column = raw[:, :passes, :].rearrange("p g (m t) -> p g t m", t=SLOTS)
    nc.vector.tensor_copy(out=dealt, in_=by_column[:, :, first_slot : first_slot + slots, :])


def side_by_side(ap):
    return ap.rearrange("p (c i) t -> p c t i", i=RUN)


def by_slot(ap):
    return ap.rearrange("p t (c i) -> p c t i", i=RUN)


def tile_picked_yleaseq_max_po_kernel(
    tc, x_words, x_scales, w1_words, w1_scales, w2_words, w2_scales, unit, w3_words, w3_scales, offs, hl, wt,
    out_0, out_1, out_2,
):
    nc = tc.nc
    with ExitStack() as ctx:
        lists = ctx.enter_context(tc.tile_pool(name="lists", bufs=1))
        keep = ctx.enter_context(tc.tile_pool(name="keep", bufs=1))
        shared = ctx.enter_context(tc.tile_pool(name="shared", bufs=1))
        holders = ctx.enter_context(tc.tile_pool(name="holders", bufs=8))
        pairs = ctx.enter_context(tc.tile_pool(name="pairs", bufs=2))
        psum = ctx.enter_context(tc.psum_pool(name="psum", bufs=8))

        offs_sb = lists.tile([P, S // 16], U16, name="offs_sb")
        hl_sb = lists.tile([P, U // 16], U16, name="hl_sb")
        wt_sb = lists.tile([P, U // 16], U16, name="wt_sb")

        x_scales_raw = keep.tile([P, PASSES, T], U8, name="x_scales_raw", align_bytes=64)
        w1_scales_raw = keep.tile([P, PASSES, N], U8, name="w1_scales_raw", align_bytes=64)
        w2_scales_raw = shared.tile([P, PASSES, N], U8, name="w2_scales_raw", align_bytes=64, offset=W2_SCALES_RAW_AT)
        nc.vector.memset(x_scales_raw[:, 0, :].bitcast(I32), 0)
        nc.gpsimd.memset(x_scales_raw[:, 1, :].bitcast(I32), 0)
        nc.gpsimd.memset(w1_scales_raw[:].bitcast(I32), 0)
        nc.gpsimd.memset(w2_scales_raw[:].bitcast(I32), 0)

        x_raw = [
            keep.tile([P, T], I32, name="x_raw0", align_bytes=64),
            shared.tile([P, T], I32, name="x_raw1", align_bytes=64, offset=X1_WINDOW_AT),
        ]
        w1_raw = keep.tile([P, PASSES, 2 * N], U8, name="w1_raw", align_bytes=64)
        w2_raw = shared.tile([P, PASSES, 2 * N], U8, name="w2_raw", align_bytes=64, offset=W2_WORDS_RAW_AT)
        unit_sb = keep.tile([P, SLOTS], F32, name="unit_sb")

        nc.sync.dma_start(offs_sb[:], offs)
        nc.sync.dma_start(out=unit_sb[:], in_=unit.rearrange("(p t) o -> p (t o)", t=SLOTS))
        load_scales(nc, x_scales_raw, x_scales)
        nc.sync.dma_start(out=x_raw[0][:], in_=x_words[0].rearrange("p n j -> p (n j)").bitcast(I32))
        load_words(nc, w1_raw, w1_words)
        load_scales(nc, w1_scales_raw, w1_scales)
        nc.sync.dma_start(out=x_raw[1][:], in_=x_words[1].rearrange("p n j -> p (n j)").bitcast(I32))
        nc.sync.dma_start(hl_sb[:], hl)
        load_words(nc, w2_raw, w2_words)
        nc.sync.dma_start(wt_sb[:], wt)
        load_scales(nc, w2_scales_raw, w2_scales)

        magnitude = keep.tile([P, SLOTS], F32, name="magnitude")
        sign = keep.tile([P, SLOTS], BF16, name="sign")
        root = keep.tile([P, SLOTS], F32, name="root")
        neg_root = keep.tile([P, SLOTS], F32, name="neg_root")
        neg_square = keep.tile([P, SLOTS], F32, name="neg_square")
        nc.scalar.activation(magnitude[:], unit_sb[:], ACT.Abs)
        nc.scalar.activation(sign[:], unit_sb[:], ACT.Sign)
        nc.scalar.activation(root[:], magnitude[:], ACT.Sqrt)
        nc.scalar.activation(neg_root[:], root[:], ACT.Copy, scale=-1.0)
        for t in range(SLOTS):
            nc.scalar.activation(neg_square[:, t : t + 1], root[:, t : t + 1], ACT.Copy, scale=neg_root[:, t : t + 1])

        def dealt_tiles(name, passes, slots, pool, words_at=None, scales_at=None):
            words = pool.tile([P, passes, slots, 2 * P], U8, name=name + "_words", align_bytes=64, offset=words_at)
            scales = pool.tile([P, passes, slots, P], U8, name=name + "_scales", align_bytes=64, offset=scales_at)
            return words, scales

        x_scale = [keep.tile([P, S], U8, name="x_scale%d" % g, align_bytes=64) for g in range(PASSES)]
        x_code = [keep.tile([P, S], U32, name="x_code%d" % g, align_bytes=64) for g in range(PASSES)]
        w1_head = dealt_tiles("w1_head", PASSES, 1, keep)
        w1_rest = dealt_tiles("w1_rest", PASSES, SLOTS - 1, shared, W1_WORDS_DEALT_AT, W1_SCALES_DEALT_AT)
        w2_all = dealt_tiles("w2_all", PASSES, SLOTS, shared, W2_WORDS_DEALT_AT, W2_SCALES_DEALT_AT)
        w3_all = dealt_tiles("w3_all", 1, SLOTS, keep)
        for g in range(PASSES):
            nc.vector.tensor_copy(x_scale[g][:], x_scales_raw[:, g, :].indirect(offs_sb[:]))
        nc.vector.tensor_copy(x_code[0][:], x_raw[0][:].bitcast(U32).indirect(offs_sb[:]))
        deal(nc, w1_head[1][:], w1_scales_raw[:], 0)
        deal(nc, w1_head[0][:].bitcast(U16), w1_raw[:].bitcast(U16), 0)
        nc.vector.tensor_copy(x_code[1][:], x_raw[1][:].bitcast(U32).indirect(offs_sb[:]))
        deal(nc, w2_all[1][:], w2_scales_raw[:], 0)
        deal(nc, w2_all[0][:].bitcast(U16), w2_raw[:].bitcast(U16), 0)
        deal(nc, w1_rest[1][:], w1_scales_raw[:], 1)
        deal(nc, w1_rest[0][:].bitcast(U16), w1_raw[:].bitcast(U16), 1)
        load_words(nc, w1_raw, w3_words)
        load_scales(nc, w1_scales_raw, w3_scales)

        def product(acc, weights, index, g, codes, code_scales, start, stop):
            nc.tensor.matmul_mx(
                out=acc,
                lhsT=weights[0][:, g, index, :].bitcast(FP4X4),
                lhsT_scale=weights[1][:, g, index, :],
                rhs=codes.bitcast(FP8X4),
                rhs_scale=code_scales,
                start=start,
                stop=stop,
            )

        y = [keep.tile([P, S], F32, name="y%d" % t) for t in range(SLOTS)]
        z = [keep.tile([P, S], F32, name="z%d" % t) for t in range(SLOTS)]

        def project(window, weights, index, factor):
            acc = psum.tile([P, S], F32, name="acc")
            for g in range(PASSES):
                product(acc[:], weights, index, g, x_code[g][:], x_scale[g][:], g == 0, g == PASSES - 1)
            nc.scalar.activation(window[:], acc[:], ACT.Copy, scale=factor)

        staged = []
        for c, (first, count, fused) in enumerate(STRETCHES):
            names = ("till", "with_holder", "with_waiter") if fused else ("till", "least")
            staged.append([keep.tile([P, SLOTS, count], F32, name="%s%d" % (name, c)) for name in names])

        def entries(c):
            first, count, fused = STRETCHES[c]
            columns = slice(first // 16, (first + count) // 16)
            return hl_sb[:, columns], wt_sb[:, columns]

        slot0_holder = shared.tile([P, U], F32, name="slot0_holder", align_bytes=64, offset=SLOT0_HOLDER_AT)

        def look_up_y(c, t):
            holder, waiter = entries(c)
            first, count, fused = STRETCHES[c]
            if t == 0:
                y_holder = slot0_holder[:, first : first + count]
            else:
                y_holder = holders.tile([P, count], F32, name="y_holder")[:]
            nc.scalar.activation(y_holder, y[t][:].indirect(holder), ACT.Copy)
            nc.vector.tensor_tensor(staged[c][0][:, t, :], y[t][:].indirect(waiter), y_holder, ALU.mult)

        def look_up_z_fused(c, t):
            holder, waiter = entries(c)
            till, with_holder, with_waiter = staged[c]
            nc.vector.tensor_tensor(with_holder[:, t, :], z[t][:].indirect(holder), till[:, t, :], ALU.add)
            nc.vector.tensor_tensor(with_waiter[:, t, :], z[t][:].indirect(waiter), till[:, t, :], ALU.add)

        def look_up_pair(c, t0):
            holder, waiter = entries(c)
            count = STRETCHES[c][1]
            if (c, t0) == (1, 0):
                fetched = shared.tile([P, 2, 2, count], F32, name="first_pair", align_bytes=64, offset=FIRST_PAIR_AT)
            else:
                fetched = pairs.tile([P, 2, 2, count], F32, name="pair")
            z_holder, z_waiter = fetched[:, 0, :, :], fetched[:, 1, :, :]
            for j in range(2):
                look_up_y(c, t0 + j)
                nc.scalar.activation(z_holder[:, j, :], z[t0 + j][:].indirect(holder), ACT.Copy)
                nc.scalar.activation(z_waiter[:, j, :], z[t0 + j][:].indirect(waiter), ACT.Copy)
            nc.vector.tensor_tensor(staged[c][1][:, t0 : t0 + 2, :], z_holder, z_waiter, ALU.min)

        out_rows = out_0.rearrange("(p t) r -> p t r", t=SLOTS)
        out_words = out_1[0].rearrange("p r j -> p (r j)").bitcast(I32)
        out_scales = keep.tile([P, U], U8, name="out_scales", align_bytes=64)
        out_codes = keep.tile([P, U], U32, name="out_codes", align_bytes=64)

        def finish(k):
            c, at, count = PIECES[k]
            first, fused = STRETCHES[c][0] + at, STRETCHES[c][2]
            left, right = [by_slot(tile[:, :, at : at + count]) for tile in staged[c][-2:]]
            unsigned = keep.tile([P, count, SLOTS], BF16, name="unsigned%d" % k, align_bytes=64)
            nc.vector.tensor_tensor(side_by_side(unsigned[:]), left, right, ALU.min if fused else ALU.add)
            hid = keep.tile([P, count, SLOTS], BF16, name="hid%d" % k, align_bytes=64)
            nc.vector.tensor_tensor(hid[:], unsigned[:], sign[:].unsqueeze(1).to_broadcast([P, count, SLOTS]), ALU.mult)
            hid_code = keep.tile([P, count], U32, name="hid_code%d" % k, align_bytes=64)
            hid_scale = keep.tile([P, count], U8, name="hid_scale%d" % k, align_bytes=64)
            nc.vector.quantize_mx(
                out=hid_code[:].bitcast(FP8X4), scales=hid_scale[:], in_=hid[:].rearrange("p r t -> p (r t)")
            )
            result = keep.tile([P, SLOTS, count], F32, name="result%d" % k)
            for start in range(0, count, BANK // 2):
                width = min(BANK // 2, count - start)
                part = slice(start, start + width)
                per_bank = BANK // width
                for t0 in range(0, SLOTS, per_bank):
                    acc = psum.tile([P, per_bank, width], F32, name="acc")
                    for j in range(per_bank):
                        product(acc[:, j, :], w3_all, t0 + j, 0, hid_code[:, part], hid_scale[:, part], True, True)
                    nc.scalar.activation(result[:, t0 : t0 + per_bank, part], acc[:], ACT.Copy)
            nc.sync.dma_start(out=out_rows[:, :, first : first + count], in_=result[:])
            return result

        rounded = keep.tile([P, U, SLOTS], BF16, name="rounded", align_bytes=64)

        def round_once(k, result):
            c, at, count = PIECES[k]
            first = STRETCHES[c][0] + at
            target = side_by_side(rounded[:, first : first + count, :])
            if k < ROUNDED_ON_SCALAR:
                nc.scalar.activation(target, by_slot(result[:]), ACT.Copy)
            else:
                nc.vector.tensor_copy(out=target, in_=by_slot(result[:]))

        def quantize_planes(first, count):
            columns = slice(first, first + count)
            nc.vector.quantize_mx(
                out=out_codes[:, columns].bitcast(FP8X4),
                scales=out_scales[:, columns],
                in_=rounded[:, columns, :].rearrange("p r t -> p (r t)"),
            )

        for t in range(SLOTS):
            weights, index = (w1_head, 0) if t == 0 else (w1_rest, t - 1)
            project(y[t], weights, index, root[:, t : t + 1])
            look_up_y(0, t)
            project(z[t], w2_all, t, neg_square[:, t : t + 1])
            look_up_z_fused(0, t)
        deal(nc, w3_all[1][:], w1_scales_raw[:], 0)
        deal(nc, w3_all[0][:].bitcast(U16), w1_raw[:].bitcast(U16), 0)
        results = []
        for c in range(len(STRETCHES)):
            if c > 0:
                for t0 in range(0, SLOTS, 2):
                    look_up_pair(c, t0)
            for k in range(len(PIECES)):
                if PIECES[k][0] == c:
                    results.append(finish(k))
        for k, result in enumerate(results):
            round_once(k, result)
            for first, count, after in PLANE_CALLS:
                if after == k:
                    quantize_planes(first, count)
        last = STRETCHES[-1][0]
        for columns in (slice(0, last), slice(last, U)):
            nc.sync.dma_start(out=out_words[:, columns], in_=out_codes[:, columns].bitcast(I32))
        for q in range(QUADRANTS):
            queue = nc.sync if q % 2 else nc.scalar
            queue.dma_start(
                out=out_2[0, 4 * q : 4 * q + 4, :].bitcast(I32), in_=out_scales[32 * q : 32 * q + 4, :].bitcast(I32)
            )
